import numpy as np
import ml_dtypes


def mxq(x, axis, fmt="e4m3"):
    dtype, down = {"e4m3": (ml_dtypes.float8_e4m3fn, 7), "e5m2": (ml_dtypes.float8_e5m2, 14)}[fmt]
    v = np.moveaxis(np.asarray(x, np.float32).astype(ml_dtypes.bfloat16).astype(np.float64), axis, -1)
    blocks = v.reshape(v.shape[:-1] + (-1, 32))
    amax = np.abs(blocks).max(-1, keepdims=True)
    byte = np.maximum(np.where(amax > 0, np.frexp(amax)[1] - 1 + 127, 0) - down, 1)
    scale = np.exp2(byte - 127.0)
    codes = (blocks / scale).astype(np.float32).astype(dtype).astype(np.float64)
    return np.moveaxis((codes * scale).reshape(v.shape), -1, axis)


WIDE = False


def mx_kscale(k):
    if not WIDE:
        return np.ones(k)
    levels = np.array([10, -10, 5, -5, 0])
    if k % 512:
        return np.exp2(np.random.permutation(np.resize(levels, k // 32))).repeat(32)
    a = np.empty((k // 512, 16))
    for p in range(k // 512):
        a[p, :8] = np.random.permutation(np.resize(levels, 8))
        for g in range(8):
            far = levels[np.abs(levels - a[p, g]) >= 10]
            a[p, g + 8] = far[np.random.randint(len(far))]
    return np.exp2(a.ravel()).repeat(32)


def f64(x):
    return np.asarray(x).astype(np.float64)


def striped8(idx):
    return np.asarray(idx).reshape(8, -1, 16).transpose(0, 2, 1).reshape(128, -1).astype(np.uint16)


def unstriped8(offs):
    return offs.reshape(8, 16, -1).transpose(0, 2, 1).reshape(8, -1).astype(np.int64)


def pick8(x, idx, run):
    r = np.arange(len(x))
    return x[r[:, None], idx[r % (8 * run) // run]]


E2M1 = np.array([0.0, 0.5, 1.0, 1.5, 2.0, 3.0, 4.0, 6.0, -0.0, -0.5, -1.0, -1.5, -2.0, -3.0, -4.0, -6.0])


def pack_weight(w, fmt):
    k, n = w.shape
    w = f64(np.asarray(w, np.float32).astype(ml_dtypes.bfloat16)).reshape(k // 32, 32, n)
    amax = np.abs(w).max(1)
    if fmt == "e4m3":
        byte = np.frexp(amax)[1] - 1 + 127 - 7
    else:
        mant, ex = np.frexp(amax / 6.0)
        byte = np.where(mant > 0.5, ex, ex - 1) + 127
    byte = np.clip(np.where(amax > 0, byte, 1), 1, 254)
    scaled = (w * np.exp2(127.0 - byte)[:, None, :]).reshape(k, n).astype(np.float32)
    by_word = np.ascontiguousarray(scaled.reshape(k // 512, 128, 4, n).transpose(0, 1, 3, 2))
    if fmt == "e4m3":
        words = by_word.astype(ml_dtypes.float8_e4m3fn).view(np.uint8)
    else:
        c = by_word.astype(ml_dtypes.float4_e2m1fn).view(np.uint8) & 0xF
        words = (c[..., 0::2] | (c[..., 1::2] << 4)).reshape(k // 512, 128, 2 * n)
    return np.ascontiguousarray(words), np.ascontiguousarray(byte.astype(np.uint8).reshape(k // 512, 16, n))


def unpack_weight(words, scales, fmt):
    g, _, n = scales.shape
    words = np.ascontiguousarray(words).reshape(g, 128, n, -1)
    if fmt == "e4m3":
        vals = words.view(ml_dtypes.float8_e4m3fn).astype(np.float64)
    else:
        nib = np.empty((g, 128, n, 4), np.uint8)
        nib[..., 0::2] = words & 0xF
        nib[..., 1::2] = words >> 4
        vals = E2M1[nib]
    vals = vals * np.repeat(np.exp2(scales.astype(np.float64) - 127.0), 8, axis=1)[..., None]
    return vals.transpose(0, 1, 3, 2).reshape(g * 512, n)


D, T, U, I, Q = 512, 1024, 1024, 512, 128


def setup_inputs():
    n = np.random.standard_normal
    idx = np.stack([np.random.permutation(T)[:I] for _ in range(8)])
    idx2 = np.stack([np.random.permutation(U)[:I] for _ in range(8)])
    idx3 = np.stack([np.random.permutation(T)[:I] for _ in range(8)])
    fd = mx_kscale(D)
    keysp = pack_weight(n((D, T)) / fd[:, None], "e4m3")
    notesp = pack_weight(n((D, U)) / fd[:, None], "e2m1")
    return {
        "query": (n((D, Q)) * 1.0 / np.sqrt(D) * fd[:, None]).astype(np.float32),
        "keys_words": keysp[0],
        "keys_scales": keysp[1],
        "notes_words": notesp[0],
        "notes_scales": notesp[1],
        "lam": (np.random.uniform(0.5, 1.5, (Q, 1))).astype(np.float32),
        "offs": striped8(idx),
        "offs2": striped8(idx2),
        "offs3": striped8(idx3),
    }


def reference(query, keys_words, keys_scales, notes_words, notes_scales, lam, offs, offs2, offs3):
    idx = unstriped8(offs)
    idx2 = unstriped8(offs2)
    idx3 = unstriped8(offs3)
    keysu = unpack_weight(keys_words, keys_scales, "e4m3")
    notesu = unpack_weight(notes_words, notes_scales, "e2m1")
    queryq = mxq(f64(query), 0, "e4m3")
    a = queryq.T @ keysu
    b = queryq.T @ notesu
    w = np.minimum(pick8(a, idx, 16), pick8(b, idx2, 16))
    f1 = np.zeros((Q, T))
    f1[np.arange(Q)[:, None], idx[np.arange(Q) % 128 // 16]] = w
    cc = a + f1 * f64(lam)
    y = pick8(cc, idx3, 16)
    return y

@@ -1,0 +1,135 @@
+from contextlib import ExitStack
+
+import concourse.mybir as mybir
+
+D, T, U, SLOTS, Q = 512, 1024, 1024, 512, 128
+FLOPS = 2 * D * Q * (T + U)
+
+F32 = mybir.dt.float32
+BF16 = mybir.dt.bfloat16
+I32 = mybir.dt.int32
+U32 = mybir.dt.uint32
+U16 = mybir.dt.uint16
+U8 = mybir.dt.uint8
+FP8X4 = mybir.dt.float8_e4m3fn_x4
+FP4X4 = mybir.dt.float4_e2m1fn_x4
+ALU = mybir.AluOpType
+COPY = mybir.ActivationFunctionType.Copy
+
+P = 128
+PACK = 4
+BANK = 512
+HALF = SLOTS // 2
+HALF_COLS = HALF // 16
+
+
+def load_scale_rows(nc, plane, scales):
+    for quad in range(4):
+        nc.sync.dma_start(
+            out=plane[32 * quad : 32 * quad + 4, :].bitcast(I32),
+            in_=scales[0, 4 * quad : 4 * quad + 4, :].bitcast(I32),
+        )
+
+
+def tile_attend_lowerof_two_kernel(
+    tc, query, keys_words, keys_scales, notes_words, notes_scales, lam, offs, offs2, offs3, out
+):
+    nc = tc.nc
+    with ExitStack() as ctx:
+        sb = ctx.enter_context(tc.tile_pool(name="sb", bufs=1))
+        psum = ctx.enter_context(tc.psum_pool(name="psum", bufs=1))
+
+        offs_t = sb.tile([P, SLOTS // 16], U16, name="offs_t")
+        offs2_t = sb.tile([P, SLOTS // 16], U16, name="offs2_t")
+        offs3_t = sb.tile([P, SLOTS // 16], U16, name="offs3_t")
+        notes_plane = sb.tile([P, U], U8, name="notes_plane", align_bytes=64)
+        keys_plane = sb.tile([P, T], U8, name="keys_plane", align_bytes=64)
+        f1 = sb.tile([P, T], F32, name="f1")
+        nc.vector.memset(notes_plane[:].bitcast(I32), 0)
+        nc.vector.memset(keys_plane[:].bitcast(I32), 0)
+        nc.vector.memset(f1[:], 0.0)
+
+        q_raw = sb.tile([P, PACK, Q], F32, name="q_raw")
+        nc.sync.dma_start(out=q_raw[:], in_=query.rearrange("(p j) q -> p j q", j=PACK))
+        load_scale_rows(nc, notes_plane, notes_scales)
+        notes_t = sb.tile([P, 2 * U], U8, name="notes_t", align_bytes=64)
+        nc.sync.dma_start(out=notes_t[:].bitcast(I32), in_=notes_words[0].bitcast(I32))
+        keys_flat = keys_words[0].rearrange("p n r -> p (n r)")
+        keys_t = []
+        for h in range(T // BANK):
+            words = sb.tile([P, BANK], U32, name="keys_t%d" % h, align_bytes=64)
+            nc.sync.dma_start(
+                out=words[:].bitcast(I32),
+                in_=keys_flat[:, PACK * BANK * h : PACK * BANK * (h + 1)].bitcast(I32),
+            )
+            keys_t.append(words)
+        load_scale_rows(nc, keys_plane, keys_scales)
+        nc.sync.dma_start(offs2_t[:], offs2)
+        nc.sync.dma_start(offs_t[:], offs)
+        nc.sync.dma_start(offs3_t[:], offs3)
+        lam_t = sb.tile([P, 1], F32, name="lam_t")
+        nc.sync.dma_start(out=lam_t[:], in_=lam)
+
+        q_bf = sb.tile([P, Q, PACK], BF16, name="q_bf", align_bytes=64)
+        nc.vector.tensor_copy(
+            out=q_bf[:].rearrange("p (c i) j -> p c j i", i=4),
+            in_=q_raw[:].rearrange("p j (c i) -> p c j i", i=4),
+        )
+        q_codes = sb.tile([P, Q], U32, name="q_codes", align_bytes=64)
+        q_plane = sb.tile([P, Q], U8, name="q_plane", align_bytes=64)
+        nc.vector.quantize_mx(
+            out=q_codes[:].bitcast(FP8X4),
+            scales=q_plane[:],
+            in_=q_bf[:].rearrange("p q j -> p (q j)"),
+        )
+
+        def score(name, words, plane):
+            bank = psum.tile([P, BANK], F32, name=name)
+            nc.tensor.matmul_mx(
+                out=bank[:],
+                lhsT=q_codes[:].bitcast(FP8X4),
+                lhsT_scale=q_plane[:],
+                rhs=words,
+                rhs_scale=plane,
+                start=True,
+                stop=True,
+            )
+            return bank
+
+        b_banks = [
+            score("b_bank%d" % h, notes_t[:, 2 * BANK * h : 2 * BANK * (h + 1)].bitcast(FP4X4),
+                  notes_plane[:, BANK * h : BANK * (h + 1)])
+            for h in range(U // BANK)
+        ]
+        a_banks = [
+            score("a_bank%d" % h, keys_t[h][:].bitcast(FP8X4), keys_plane[:, BANK * h : BANK * (h + 1)])
+            for h in range(T // BANK)
+        ]
+
+        a = sb.tile([P, T], F32, name="a")
+        b = sb.tile([P, U], F32, name="b")
+        nc.vector.tensor_copy(out=b[:, 0:BANK], in_=b_banks[0][:])
+        nc.scalar.activation(b[:, BANK:U], b_banks[1][:], COPY)
+        nc.vector.tensor_copy(out=a[:, 0:BANK], in_=a_banks[0][:])
+        nc.vector.tensor_copy(out=a[:, BANK:T], in_=a_banks[1][:])
+
+        cols = [slice(HALF_COLS * s, HALF_COLS * (s + 1)) for s in range(2)]
+        ga = [sb.tile([P, HALF], F32, name="ga%d" % s) for s in range(2)]
+        gb = [sb.tile([P, HALF], F32, name="gb%d" % s) for s in range(2)]
+        w = [sb.tile([P, HALF], F32, name="w%d" % s) for s in range(2)]
+        nc.scalar.activation(gb[0][:], b[:].indirect(offs2_t[:, cols[0]]), COPY)
+        nc.scalar.activation(gb[1][:], b[:].indirect(offs2_t[:, cols[1]]), COPY)
+        nc.vector.tensor_copy(ga[0][:], a[:].indirect(offs_t[:, cols[0]]))
+        nc.scalar.activation(ga[1][:], a[:].indirect(offs_t[:, cols[1]]), COPY)
+        for s in range(2):
+            nc.vector.tensor_tensor(w[s][:], ga[s][:], gb[s][:], ALU.min)
+            nc.vector.tensor_copy(f1[:].indirect(offs_t[:, cols[s]]), w[s][:])
+
+        cc = sb.tile([P, T], F32, name="cc")
+        nc.vector.scalar_tensor_tensor(cc[:], f1[:], lam_t[:], a[:], ALU.mult, ALU.add)
+
+        y = [sb.tile([P, HALF], F32, name="y%d" % s) for s in range(2)]
+        nc.vector.tensor_copy(y[0][:], cc[:].indirect(offs3_t[:, cols[0]]))
+        nc.scalar.activation(y[1][:], cc[:].indirect(offs3_t[:, cols[1]]), COPY)
+        for s in range(2):
+            nc.sync.dma_start(out=out[:, HALF * s : HALF * (s + 1)], in_=y[s][:])

@@ -23,8 +23,8 @@ HALF = SLOTS // 2
 HALF_COLS = HALF // 16
 
 
-def load_scale_rows(nc, plane, scales):
-    for quad in range(4):
+def load_scale_rows(nc, plane, scales, quads):
+    for quad in quads:
         nc.sync.dma_start(
             out=plane[32 * quad : 32 * quad + 4, :].bitcast(I32),
             in_=scales[0, 4 * quad : 4 * quad + 4, :].bitcast(I32),
@@ -51,19 +51,13 @@ def tile_attend_lowerof_two_kernel(
 
         q_raw = sb.tile([P, PACK, Q], F32, name="q_raw")
         nc.sync.dma_start(out=q_raw[:], in_=query.rearrange("(p j) q -> p j q", j=PACK))
-        load_scale_rows(nc, notes_plane, notes_scales)
+        load_scale_rows(nc, notes_plane, notes_scales, (0, 1))
         notes_t = sb.tile([P, 2 * U], U8, name="notes_t", align_bytes=64)
         nc.sync.dma_start(out=notes_t[:].bitcast(I32), in_=notes_words[0].bitcast(I32))
-        keys_flat = keys_words[0].rearrange("p n r -> p (n r)")
-        keys_t = []
-        for h in range(T // BANK):
-            words = sb.tile([P, BANK], U32, name="keys_t%d" % h, align_bytes=64)
-            nc.sync.dma_start(
-                out=words[:].bitcast(I32),
-                in_=keys_flat[:, PACK * BANK * h : PACK * BANK * (h + 1)].bitcast(I32),
-            )
-            keys_t.append(words)
-        load_scale_rows(nc, keys_plane, keys_scales)
+        load_scale_rows(nc, notes_plane, notes_scales, (2, 3))
+        keys_t = sb.tile([P, T], U32, name="keys_t", align_bytes=64)
+        nc.sync.dma_start(out=keys_t[:].bitcast(I32), in_=keys_words[0].rearrange("p n r -> p (n r)").bitcast(I32))
+        load_scale_rows(nc, keys_plane, keys_scales, (0, 1, 2, 3))
         nc.sync.dma_start(offs2_t[:], offs2)
         nc.sync.dma_start(offs_t[:], offs)
         nc.sync.dma_start(offs3_t[:], offs3)
@@ -71,10 +65,11 @@ def tile_attend_lowerof_two_kernel(
         nc.sync.dma_start(out=lam_t[:], in_=lam)
 
         q_bf = sb.tile([P, Q, PACK], BF16, name="q_bf", align_bytes=64)
-        nc.vector.tensor_copy(
-            out=q_bf[:].rearrange("p (c i) j -> p c j i", i=4),
-            in_=q_raw[:].rearrange("p j (c i) -> p c j i", i=4),
-        )
+        for copy, rows in ((nc.vector.tensor_copy, slice(0, Q // 2)), (nc.scalar.copy, slice(Q // 2, Q))):
+            copy(
+                out=q_bf[:, rows, :].rearrange("p (c i) j -> p c j i", i=4),
+                in_=q_raw[:, :, rows].rearrange("p j (c i) -> p c j i", i=4),
+            )
         q_codes = sb.tile([P, Q], U32, name="q_codes", align_bytes=64)
         q_plane = sb.tile([P, Q], U8, name="q_plane", align_bytes=64)
         nc.vector.quantize_mx(
@@ -84,7 +79,7 @@ def tile_attend_lowerof_two_kernel(
         )
 
         def score(name, words, plane):
-            bank = psum.tile([P, BANK], F32, name=name)
+            bank = psum.tile([P, plane.shape[1]], F32, name=name)
             nc.tensor.matmul_mx(
                 out=bank[:],
                 lhsT=q_codes[:].bitcast(FP8X4),
@@ -101,25 +96,26 @@ def tile_attend_lowerof_two_kernel(
                   notes_plane[:, BANK * h : BANK * (h + 1)])
             for h in range(U // BANK)
         ]
+        a_cuts = (0, 512, 768, 1024)
         a_banks = [
-            score("a_bank%d" % h, keys_t[h][:].bitcast(FP8X4), keys_plane[:, BANK * h : BANK * (h + 1)])
-            for h in range(T // BANK)
+            score("a_bank%d" % lo, keys_t[:, lo:hi].bitcast(FP8X4), keys_plane[:, lo:hi])
+            for lo, hi in zip(a_cuts, a_cuts[1:])
         ]
 
         a = sb.tile([P, T], F32, name="a")
         b = sb.tile([P, U], F32, name="b")
-        nc.vector.tensor_copy(out=b[:, 0:BANK], in_=b_banks[0][:])
-        nc.scalar.activation(b[:, BANK:U], b_banks[1][:], COPY)
-        nc.vector.tensor_copy(out=a[:, 0:BANK], in_=a_banks[0][:])
-        nc.vector.tensor_copy(out=a[:, BANK:T], in_=a_banks[1][:])
-
         cols = [slice(HALF_COLS * s, HALF_COLS * (s + 1)) for s in range(2)]
         ga = [sb.tile([P, HALF], F32, name="ga%d" % s) for s in range(2)]
-        gb = [sb.tile([P, HALF], F32, name="gb%d" % s) for s in range(2)]
         w = [sb.tile([P, HALF], F32, name="w%d" % s) for s in range(2)]
-        nc.scalar.activation(gb[0][:], b[:].indirect(offs2_t[:, cols[0]]), COPY)
-        nc.scalar.activation(gb[1][:], b[:].indirect(offs2_t[:, cols[1]]), COPY)
+        gb = [sb.tile([P, HALF], F32, name="gb0"), sb.tile([P, HALF], F32, name="gb1", tag="keys_t", align_bytes=64)]
+        nc.vector.tensor_copy(out=b[:, 0:BANK], in_=b_banks[0][:])
+        nc.scalar.activation(b[:, BANK:U], b_banks[1][:], COPY)
+        nc.vector.tensor_copy(gb[0][:], b[:].indirect(offs2_t[:, cols[0]]))
+        nc.scalar.activation(a[:, 0:512], a_banks[0][:], COPY)
+        nc.vector.tensor_copy(out=a[:, 512:768], in_=a_banks[1][:])
+        nc.scalar.activation(a[:, 768:1024], a_banks[2][:], COPY)
         nc.vector.tensor_copy(ga[0][:], a[:].indirect(offs_t[:, cols[0]]))
+        nc.scalar.activation(gb[1][:], b[:].indirect(offs2_t[:, cols[1]]), COPY)
         nc.scalar.activation(ga[1][:], a[:].indirect(offs_t[:, cols[1]]), COPY)
         for s in range(2):
             nc.vector.tensor_tensor(w[s][:], ga[s][:], gb[s][:], ALU.min)
@@ -131,5 +127,5 @@ def tile_attend_lowerof_two_kernel(
         y = [sb.tile([P, HALF], F32, name="y%d" % s) for s in range(2)]
         nc.vector.tensor_copy(y[0][:], cc[:].indirect(offs3_t[:, cols[0]]))
         nc.scalar.activation(y[1][:], cc[:].indirect(offs3_t[:, cols[1]]), COPY)
-        for s in range(2):
-            nc.sync.dma_start(out=out[:, HALF * s : HALF * (s + 1)], in_=y[s][:])
+        nc.sync.dma_start(out=out[:, 0:HALF], in_=y[0][:])
+        nc.scalar.dma_start(out=out[:, HALF:SLOTS], in_=y[1][:])

from contextlib import ExitStack

import concourse.mybir as mybir

D, T, U, SLOTS, Q = 512, 1024, 1024, 512, 128
FLOPS = 2 * D * Q * (T + U)

F32 = mybir.dt.float32
BF16 = mybir.dt.bfloat16
I32 = mybir.dt.int32
U32 = mybir.dt.uint32
U16 = mybir.dt.uint16
U8 = mybir.dt.uint8
FP8X4 = mybir.dt.float8_e4m3fn_x4
FP4X4 = mybir.dt.float4_e2m1fn_x4
ALU = mybir.AluOpType
COPY = mybir.ActivationFunctionType.Copy

P = 128
PACK = 4
BANK = 512
HALF = SLOTS // 2
HALF_COLS = HALF // 16


def load_scale_rows(nc, plane, scales, quads):
    for quad in quads:
        nc.sync.dma_start(
            out=plane[32 * quad : 32 * quad + 4, :].bitcast(I32),
            in_=scales[0, 4 * quad : 4 * quad + 4, :].bitcast(I32),
        )


def tile_attend_lowerof_two_kernel(
    tc, query, keys_words, keys_scales, notes_words, notes_scales, lam, offs, offs2, offs3, out
):
    nc = tc.nc
    with ExitStack() as ctx:
        sb = ctx.enter_context(tc.tile_pool(name="sb", bufs=1))
        psum = ctx.enter_context(tc.psum_pool(name="psum", bufs=1))

        offs_t = sb.tile([P, SLOTS // 16], U16, name="offs_t")
        offs2_t = sb.tile([P, SLOTS // 16], U16, name="offs2_t")
        offs3_t = sb.tile([P, SLOTS // 16], U16, name="offs3_t")
        notes_plane = sb.tile([P, U], U8, name="notes_plane", align_bytes=64)
        keys_plane = sb.tile([P, T], U8, name="keys_plane", align_bytes=64)
        f1 = sb.tile([P, T], F32, name="f1")
        nc.vector.memset(notes_plane[:].bitcast(I32), 0)
        nc.vector.memset(keys_plane[:].bitcast(I32), 0)
        nc.vector.memset(f1[:], 0.0)

        q_raw = sb.tile([P, PACK, Q], F32, name="q_raw")
        nc.sync.dma_start(out=q_raw[:], in_=query.rearrange("(p j) q -> p j q", j=PACK))
        load_scale_rows(nc, notes_plane, notes_scales, (0, 1))
        notes_t = sb.tile([P, 2 * U], U8, name="notes_t", align_bytes=64)
        nc.sync.dma_start(out=notes_t[:].bitcast(I32), in_=notes_words[0].bitcast(I32))
        load_scale_rows(nc, notes_plane, notes_scales, (2, 3))
        keys_t = sb.tile([P, T], U32, name="keys_t", align_bytes=64)
        nc.sync.dma_start(out=keys_t[:].bitcast(I32), in_=keys_words[0].rearrange("p n r -> p (n r)").bitcast(I32))
        load_scale_rows(nc, keys_plane, keys_scales, (0, 1, 2, 3))
        nc.sync.dma_start(offs2_t[:], offs2)
        nc.sync.dma_start(offs_t[:], offs)
        nc.sync.dma_start(offs3_t[:], offs3)
        lam_t = sb.tile([P, 1], F32, name="lam_t")
        nc.sync.dma_start(out=lam_t[:], in_=lam)

        q_bf = sb.tile([P, Q, PACK], BF16, name="q_bf", align_bytes=64)
        for copy, rows in ((nc.vector.tensor_copy, slice(0, Q // 2)), (nc.scalar.copy, slice(Q // 2, Q))):
            copy(
                out=q_bf[:, rows, :].rearrange("p (c i) j -> p c j i", i=4),
                in_=q_raw[:, :, rows].rearrange("p j (c i) -> p c j i", i=4),
            )
        q_codes = sb.tile([P, Q], U32, name="q_codes", align_bytes=64)
        q_plane = sb.tile([P, Q], U8, name="q_plane", align_bytes=64)
        nc.vector.quantize_mx(
            out=q_codes[:].bitcast(FP8X4),
            scales=q_plane[:],
            in_=q_bf[:].rearrange("p q j -> p (q j)"),
        )

        def score(name, words, plane):
            bank = psum.tile([P, plane.shape[1]], F32, name=name)
            nc.tensor.matmul_mx(
                out=bank[:],
                lhsT=q_codes[:].bitcast(FP8X4),
                lhsT_scale=q_plane[:],
                rhs=words,
                rhs_scale=plane,
                start=True,
                stop=True,
            )
            return bank

        b_banks = [
            score("b_bank%d" % h, notes_t[:, 2 * BANK * h : 2 * BANK * (h + 1)].bitcast(FP4X4),
                  notes_plane[:, BANK * h : BANK * (h + 1)])
            for h in range(U // BANK)
        ]
        a_cuts = (0, 512, 768, 1024)
        a_banks = [
            score("a_bank%d" % lo, keys_t[:, lo:hi].bitcast(FP8X4), keys_plane[:, lo:hi])
            for lo, hi in zip(a_cuts, a_cuts[1:])
        ]

        a = sb.tile([P, T], F32, name="a")
        b = sb.tile([P, U], F32, name="b")
        cols = [slice(HALF_COLS * s, HALF_COLS * (s + 1)) for s in range(2)]
        ga = [sb.tile([P, HALF], F32, name="ga%d" % s) for s in range(2)]
        w = [sb.tile([P, HALF], F32, name="w%d" % s) for s in range(2)]
        gb = [sb.tile([P, HALF], F32, name="gb0"), sb.tile([P, HALF], F32, name="gb1", tag="keys_t", align_bytes=64)]
        nc.vector.tensor_copy(out=b[:, 0:BANK], in_=b_banks[0][:])
        nc.scalar.activation(b[:, BANK:U], b_banks[1][:], COPY)
        nc.vector.tensor_copy(gb[0][:], b[:].indirect(offs2_t[:, cols[0]]))
        nc.scalar.activation(a[:, 0:512], a_banks[0][:], COPY)
        nc.vector.tensor_copy(out=a[:, 512:768], in_=a_banks[1][:])
        nc.scalar.activation(a[:, 768:1024], a_banks[2][:], COPY)
        nc.vector.tensor_copy(ga[0][:], a[:].indirect(offs_t[:, cols[0]]))
        nc.scalar.activation(gb[1][:], b[:].indirect(offs2_t[:, cols[1]]), COPY)
        nc.scalar.activation(ga[1][:], a[:].indirect(offs_t[:, cols[1]]), COPY)
        for s in range(2):
            nc.vector.tensor_tensor(w[s][:], ga[s][:], gb[s][:], ALU.min)
            nc.vector.tensor_copy(f1[:].indirect(offs_t[:, cols[s]]), w[s][:])

        cc = sb.tile([P, T], F32, name="cc")
        nc.vector.scalar_tensor_tensor(cc[:], f1[:], lam_t[:], a[:], ALU.mult, ALU.add)

        y = [sb.tile([P, HALF], F32, name="y%d" % s) for s in range(2)]
        nc.vector.tensor_copy(y[0][:], cc[:].indirect(offs3_t[:, cols[0]]))
        nc.scalar.activation(y[1][:], cc[:].indirect(offs3_t[:, cols[1]]), COPY)
        nc.sync.dma_start(out=out[:, 0:HALF], in_=y[0][:])
        nc.scalar.dma_start(out=out[:, HALF:SLOTS], in_=y[1][:])
